import numpy as np
import ml_dtypes


def mxq(x, axis, fmt="e4m3"):
    dtype, down = {"e4m3": (ml_dtypes.float8_e4m3fn, 7), "e5m2": (ml_dtypes.float8_e5m2, 14)}[fmt]
    v = np.moveaxis(np.asarray(x, np.float32).astype(ml_dtypes.bfloat16).astype(np.float64), axis, -1)
    blocks = v.reshape(v.shape[:-1] + (-1, 32))
    amax = np.abs(blocks).max(-1, keepdims=True)
    byte = np.maximum(np.where(amax > 0, np.frexp(amax)[1] - 1 + 127, 0) - down, 1)
    scale = np.exp2(byte - 127.0)
    codes = (blocks / scale).astype(np.float32).astype(dtype).astype(np.float64)
    return np.moveaxis((codes * scale).reshape(v.shape), -1, axis)


WIDE = False


def mx_kscale(k):
    if not WIDE:
        return np.ones(k)
    levels = np.array([10, -10, 5, -5, 0])
    if k % 512:
        return np.exp2(np.random.permutation(np.resize(levels, k // 32))).repeat(32)
    a = np.empty((k // 512, 16))
    for p in range(k // 512):
        a[p, :8] = np.random.permutation(np.resize(levels, 8))
        for g in range(8):
            far = levels[np.abs(levels - a[p, g]) >= 10]
            a[p, g + 8] = far[np.random.randint(len(far))]
    return np.exp2(a.ravel()).repeat(32)


def f64(x):
    return np.asarray(x).astype(np.float64)


def striped(idx):
    return np.tile(np.asarray(idx).reshape(-1, 16).T, (8, 1)).astype(np.uint16)


def unstriped(offs):
    return offs[:16].T.reshape(-1).astype(np.int64)


B, N, T, D, NQ = 1, 512, 2048, 512, 256


def setup_inputs():
    n = np.random.standard_normal
    idx = np.random.permutation(T)[:B * N]
    idx2 = np.random.permutation(1024)[:B * N]
    s = mx_kscale(D)[:, None]
    return {
        "qT": (n((B, D, NQ)) * s * (6.00 / np.sqrt(D))).astype(np.float32),
        "kT": (np.clip(np.round(n((D, T)) * 16), -64, 64) / 16 / s).astype(np.float32),
        "gT": (np.random.randint(0, 65, (D, 1024)) / 64.0).astype(np.float32),
        "offs": striped(idx),
        "offs2": striped(idx2),
    }


def reference(qT, kT, gT, offs, offs2):
    idx = unstriped(offs)
    idx2 = unstriped(offs2)
    pick = lambda x, which: x[:, which].reshape(x.shape[0], B, -1).transpose(1, 0, 2)
    kg = pick(f64(kT), idx)
    gg = pick(f64(gT), idx2)
    ug = mxq(kg * gg, 1, "e4m3")
    qq = mxq(f64(qT), 1, "e4m3")
    a = qq.transpose(0, 2, 1) @ ug
    y = 15.0 * np.tanh(a / 15.0)
    return y

@@ -1,0 +1,135 @@
+from contextlib import ExitStack
+
+import concourse.mybir as mybir
+
+D, T, G, N, NQ = 512, 2048, 1024, 512, 256
+FLOPS = 2 * D * N * NQ
+
+F32 = mybir.dt.float32
+BF16 = mybir.dt.bfloat16
+U32 = mybir.dt.uint32
+U16 = mybir.dt.uint16
+U8 = mybir.dt.uint8
+FP8X4 = mybir.dt.float8_e4m3fn_x4
+MULT = mybir.AluOpType.mult
+TANH = mybir.ActivationFunctionType.Tanh
+
+P = 128
+PACK = 4
+CAP = 15.0
+PIECES = 4
+W = N // PIECES
+QB = NQ // P
+
+
+def tile_attend_pre_gatekey_f_topk_kernel(tc, qT, kT, gT, offs, offs2, out):
+    nc = tc.nc
+    with ExitStack() as ctx:
+        pool = ctx.enter_context(tc.tile_pool(name="pool", bufs=1))
+        psum = ctx.enter_context(tc.psum_pool(name="psum", bufs=1))
+
+        key_list = pool.tile([P, N // 16], U16, name="key_list")
+        gate_list = pool.tile([P, N // 16], U16, name="gate_list")
+        k_rows = kT.rearrange("(p t) n -> p t n", t=PACK)
+        g_rows = gT.rearrange("(p t) n -> p t n", t=PACK)
+        k_plane = [pool.tile([P, T], F32, name="k_plane%d" % t) for t in range(PACK)]
+        g_plane = [pool.tile([P, G], F32, name="g_plane%d" % t) for t in range(PACK)]
+        q_raw = pool.tile([P, PACK, NQ], F32, name="q_raw")
+
+        nc.sync.dma_start(g_plane[0][:], g_rows[:, 0, :])
+        nc.sync.dma_start(gate_list[:], offs2)
+        nc.sync.dma_start(key_list[:], offs)
+        nc.sync.dma_start(k_plane[0][:], k_rows[:, 0, :])
+        nc.sync.dma_start(q_raw[:], qT[0].rearrange("(p t) q -> p t q", t=PACK))
+        for t in range(1, PACK):
+            nc.sync.dma_start(g_plane[t][:], g_rows[:, t, :])
+            nc.sync.dma_start(k_plane[t][:], k_rows[:, t, :])
+
+        zero = pool.tile([P, 1], F32, name="zero")
+        zero_bias = pool.tile([P, 1], F32, name="zero_bias")
+        nc.vector.memset(zero[:], 0.0)
+        nc.scalar.activation(zero_bias[:], zero[:], TANH)
+
+        gates = [pool.tile([P, N], F32, name="gates%d" % t) for t in range(PACK)]
+        u_low = pool.tile([P, 2, N], F32, name="u_low")
+        u_high = [pool.tile([P, 2, W], F32, name="u_high%d" % j) for j in range(PIECES)]
+        u_woven = [pool.tile([P, W, PACK], BF16, name="u_woven%d" % j, align_bytes=64) for j in range(PIECES)]
+
+        def gather_gates(t):
+            nc.vector.tensor_copy(gates[t][:], g_plane[t][:].indirect(gate_list[:]))
+
+        def gather_high(t, j):
+            cols = slice(j * W, (j + 1) * W)
+            entries = key_list[:, j * W // 16 : (j + 1) * W // 16]
+            nc.vector.tensor_tensor(u_high[j][:, t - 2, :], k_plane[t][:].indirect(entries), gates[t][:, cols], MULT)
+
+        gather_gates(0)
+        nc.vector.tensor_tensor(u_low[:, 0, :], k_plane[0][:].indirect(key_list[:]), gates[0][:], MULT)
+
+        q_woven = pool.tile([P, NQ, PACK], BF16, name="q_woven", align_bytes=64)
+        q_codes = pool.tile([P, NQ], U32, name="q_codes", align_bytes=64)
+        q_scales = pool.tile([P, NQ], U8, name="q_scales", align_bytes=64)
+        nc.scalar.copy(q_woven[:], q_raw[:].rearrange("p t q -> p q t"))
+
+        gather_gates(1)
+        nc.vector.quantize_mx(
+            out=q_codes[:].bitcast(FP8X4), scales=q_scales[:], in_=q_woven[:].rearrange("p q t -> p (q t)")
+        )
+        nc.vector.tensor_tensor(u_low[:, 1, :], k_plane[1][:].indirect(key_list[:]), gates[1][:], MULT)
+        for j in range(PIECES):
+            cols = slice(j * W, (j + 1) * W)
+            nc.scalar.copy(u_woven[j][:, :, 0:2], u_low[:, :, cols].rearrange("p t c -> p c t"))
+
+        gather_gates(2)
+        for j in range(PIECES):
+            gather_high(2, j)
+        gather_gates(3)
+
+        u_codes = [pool.tile([P, W], U32, name="u_codes%d" % j, align_bytes=64) for j in range(PIECES)]
+        u_scales = [pool.tile([P, W], U8, name="u_scales%d" % j, align_bytes=64) for j in range(PIECES)]
+        scores = [psum.tile([P, QB, W], F32, name="scores%d" % j) for j in range(PIECES)]
+        capped = [pool.tile([P, QB, W], F32, name="capped%d" % j) for j in range(PIECES)]
+        result = [pool.tile([P, QB, W], F32, name="result%d" % j) for j in range(PIECES)]
+        out_rows = out[0].rearrange("(b p) n -> p b n", p=P)
+
+        def weave(j, copy):
+            copy(u_woven[j][:, :, 2:4], u_high[j][:].rearrange("p t c -> p c t"))
+
+        def multiply(j):
+            nc.vector.quantize_mx(
+                out=u_codes[j][:].bitcast(FP8X4),
+                scales=u_scales[j][:],
+                in_=u_woven[j][:].rearrange("p c t -> p (c t)"),
+            )
+            for b in range(QB):
+                rows = slice(b * P, (b + 1) * P)
+                nc.tensor.matmul_mx(
+                    out=scores[j][:, b, :],
+                    lhsT=q_codes[:, rows].bitcast(FP8X4),
+                    lhsT_scale=q_scales[:, rows],
+                    rhs=u_codes[j][:].bitcast(FP8X4),
+                    rhs_scale=u_scales[j][:],
+                    start=True,
+                    stop=True,
+                )
+
+        def cap(j):
+            nc.scalar.activation(capped[j][:], scores[j][:], TANH, bias=zero_bias[:], scale=1.0 / CAP)
+
+        def store(j):
+            nc.vector.tensor_scalar_mul(result[j][:], capped[j][:], CAP)
+            nc.sync.dma_start(out_rows[:, :, j * W : (j + 1) * W], result[j][:])
+
+        for j in range(PIECES - 1):
+            gather_high(3, j)
+            weave(j, nc.scalar.copy)
+        multiply(0)
+        gather_high(3, PIECES - 1)
+        multiply(1)
+        weave(PIECES - 1, nc.vector.tensor_copy)
+        multiply(2)
+        multiply(3)
+        for j in range(PIECES):
+            cap(j)
+        for j in range(PIECES):
+            store(j)

@@ -17,8 +17,10 @@ TANH = mybir.ActivationFunctionType.Tanh
 P = 128
 PACK = 4
 CAP = 15.0
-PIECES = 4
-W = N // PIECES
+WIDTHS = [128,128,128,64,64]
+PIECES = len(WIDTHS)
+STARTS = [sum(WIDTHS[:j]) for j in range(PIECES)]
+HELD = [[0,3],[1,4]]
 QB = NQ // P
 
 
@@ -33,16 +35,16 @@ def tile_attend_pre_gatekey_f_topk_kernel(tc, qT, kT, gT, offs, offs2, out):
         k_rows = kT.rearrange("(p t) n -> p t n", t=PACK)
         g_rows = gT.rearrange("(p t) n -> p t n", t=PACK)
         k_plane = [pool.tile([P, T], F32, name="k_plane%d" % t) for t in range(PACK)]
-        g_plane = [pool.tile([P, G], F32, name="g_plane%d" % t) for t in range(PACK)]
+        g_pair = [pool.tile([P, 2, G], F32, name="g_pair%d" % h) for h in range(2)]
         q_raw = pool.tile([P, PACK, NQ], F32, name="q_raw")
 
-        nc.sync.dma_start(g_plane[0][:], g_rows[:, 0, :])
+        nc.sync.dma_start(g_pair[0][:], g_rows[:, 0:2, :])
         nc.sync.dma_start(gate_list[:], offs2)
         nc.sync.dma_start(key_list[:], offs)
         nc.sync.dma_start(k_plane[0][:], k_rows[:, 0, :])
+        nc.sync.dma_start(g_pair[1][:], g_rows[:, 2:4, :])
         nc.sync.dma_start(q_raw[:], qT[0].rearrange("(p t) q -> p t q", t=PACK))
         for t in range(1, PACK):
-            nc.sync.dma_start(g_plane[t][:], g_rows[:, t, :])
             nc.sync.dma_start(k_plane[t][:], k_rows[:, t, :])
 
         zero = pool.tile([P, 1], F32, name="zero")
@@ -52,18 +54,27 @@ def tile_attend_pre_gatekey_f_topk_kernel(tc, qT, kT, gT, offs, offs2, out):
 
         gates = [pool.tile([P, N], F32, name="gates%d" % t) for t in range(PACK)]
         u_low = pool.tile([P, 2, N], F32, name="u_low")
-        u_high = [pool.tile([P, 2, W], F32, name="u_high%d" % j) for j in range(PIECES)]
-        u_woven = [pool.tile([P, W, PACK], BF16, name="u_woven%d" % j, align_bytes=64) for j in range(PIECES)]
+        u_high = {}
+        for i, j in HELD:
+            shared = pool.tile([P, 3, WIDTHS[i]], F32, name="u_shared%d" % i)
+            u_high[i] = shared[:, 1:3, :]
+            u_high[j] = shared[:, 0:2, 0 : WIDTHS[j]]
+        for j in range(PIECES):
+            if j not in u_high:
+                alone = pool.tile([P, 2, WIDTHS[j]], F32, name="u_alone%d" % j)
+                u_high[j] = alone[:]
+        u_woven = [pool.tile([P, WIDTHS[j], PACK], BF16, name="u_woven%d" % j, align_bytes=64) for j in range(PIECES)]
 
         def gather_gates(t):
-            nc.vector.tensor_copy(gates[t][:], g_plane[t][:].indirect(gate_list[:]))
+            nc.vector.tensor_copy(gates[t][:], g_pair[t // 2][:, t % 2, :].indirect(gate_list[:]))
 
         def gather_high(t, j):
-            cols = slice(j * W, (j + 1) * W)
-            entries = key_list[:, j * W // 16 : (j + 1) * W // 16]
+            cols = slice(STARTS[j], STARTS[j] + WIDTHS[j])
+            entries = key_list[:, STARTS[j] // 16 : (STARTS[j] + WIDTHS[j]) // 16]
             nc.vector.tensor_tensor(u_high[j][:, t - 2, :], k_plane[t][:].indirect(entries), gates[t][:, cols], MULT)
 
         gather_gates(0)
+        gather_gates(1)
         nc.vector.tensor_tensor(u_low[:, 0, :], k_plane[0][:].indirect(key_list[:]), gates[0][:], MULT)
 
         q_woven = pool.tile([P, NQ, PACK], BF16, name="q_woven", align_bytes=64)
@@ -71,29 +82,28 @@ def tile_attend_pre_gatekey_f_topk_kernel(tc, qT, kT, gT, offs, offs2, out):
         q_scales = pool.tile([P, NQ], U8, name="q_scales", align_bytes=64)
         nc.scalar.copy(q_woven[:], q_raw[:].rearrange("p t q -> p q t"))
 
-        gather_gates(1)
+        gather_gates(2)
+        gather_gates(3)
         nc.vector.quantize_mx(
             out=q_codes[:].bitcast(FP8X4), scales=q_scales[:], in_=q_woven[:].rearrange("p q t -> p (q t)")
         )
         nc.vector.tensor_tensor(u_low[:, 1, :], k_plane[1][:].indirect(key_list[:]), gates[1][:], MULT)
         for j in range(PIECES):
-            cols = slice(j * W, (j + 1) * W)
+            cols = slice(STARTS[j], STARTS[j] + WIDTHS[j])
             nc.scalar.copy(u_woven[j][:, :, 0:2], u_low[:, :, cols].rearrange("p t c -> p c t"))
 
-        gather_gates(2)
         for j in range(PIECES):
             gather_high(2, j)
-        gather_gates(3)
 
-        u_codes = [pool.tile([P, W], U32, name="u_codes%d" % j, align_bytes=64) for j in range(PIECES)]
-        u_scales = [pool.tile([P, W], U8, name="u_scales%d" % j, align_bytes=64) for j in range(PIECES)]
-        scores = [psum.tile([P, QB, W], F32, name="scores%d" % j) for j in range(PIECES)]
-        capped = [pool.tile([P, QB, W], F32, name="capped%d" % j) for j in range(PIECES)]
-        result = [pool.tile([P, QB, W], F32, name="result%d" % j) for j in range(PIECES)]
+        u_codes = [pool.tile([P, WIDTHS[j]], U32, name="u_codes%d" % j, align_bytes=64) for j in range(PIECES)]
+        u_scales = [pool.tile([P, WIDTHS[j]], U8, name="u_scales%d" % j, align_bytes=64) for j in range(PIECES)]
+        scores = [psum.tile([P, QB, WIDTHS[j]], F32, name="scores%d" % j) for j in range(PIECES)]
+        capped = [pool.tile([P, QB, WIDTHS[j]], F32, name="capped%d" % j) for j in range(PIECES)]
+        result = [pool.tile([P, QB, WIDTHS[j]], F32, name="result%d" % j) for j in range(PIECES)]
         out_rows = out[0].rearrange("(b p) n -> p b n", p=P)
 
         def weave(j, copy):
-            copy(u_woven[j][:, :, 2:4], u_high[j][:].rearrange("p t c -> p c t"))
+            copy(u_woven[j][:, :, 2:4], u_high[j].rearrange("p t c -> p c t"))
 
         def multiply(j):
             nc.vector.quantize_mx(
@@ -118,18 +128,30 @@ def tile_attend_pre_gatekey_f_topk_kernel(tc, qT, kT, gT, offs, offs2, out):
 
         def store(j):
             nc.vector.tensor_scalar_mul(result[j][:], capped[j][:], CAP)
-            nc.sync.dma_start(out_rows[:, :, j * W : (j + 1) * W], result[j][:])
+            nc.sync.dma_start(out_rows[:, :, STARTS[j] : STARTS[j] + WIDTHS[j]], result[j][:])
 
-        for j in range(PIECES - 1):
-            gather_high(3, j)
-            weave(j, nc.scalar.copy)
+        gather_high(3, 0)
+        weave(0, nc.scalar.copy)
+        gather_high(3, 1)
+        weave(1, nc.scalar.copy)
+        gather_high(3, 2)
+        weave(2, nc.scalar.copy)
         multiply(0)
-        gather_high(3, PIECES - 1)
+        gather_high(3, 3)
+        weave(3, nc.scalar.copy)
         multiply(1)
-        weave(PIECES - 1, nc.vector.tensor_copy)
+        gather_high(3, 4)
+        weave(4, nc.vector.tensor_copy)
         multiply(2)
         multiply(3)
-        for j in range(PIECES):
-            cap(j)
-        for j in range(PIECES):
-            store(j)
+        multiply(4)
+        cap(0)
+        cap(1)
+        cap(2)
+        cap(3)
+        cap(4)
+        store(0)
+        store(1)
+        store(2)
+        store(3)
+        store(4)

@@ -17,10 +17,8 @@ TANH = mybir.ActivationFunctionType.Tanh
 P = 128
 PACK = 4
 CAP = 15.0
-WIDTHS = [128,128,128,64,64]
-PIECES = len(WIDTHS)
-STARTS = [sum(WIDTHS[:j]) for j in range(PIECES)]
-HELD = [[0,3],[1,4]]
+PIECES = 4
+W = N // PIECES
 QB = NQ // P
 
 
@@ -43,9 +41,9 @@ def tile_attend_pre_gatekey_f_topk_kernel(tc, qT, kT, gT, offs, offs2, out):
         nc.sync.dma_start(key_list[:], offs)
         nc.sync.dma_start(k_plane[0][:], k_rows[:, 0, :])
         nc.sync.dma_start(g_pair[1][:], g_rows[:, 2:4, :])
-        nc.sync.dma_start(q_raw[:], qT[0].rearrange("(p t) q -> p t q", t=PACK))
         for t in range(1, PACK):
             nc.sync.dma_start(k_plane[t][:], k_rows[:, t, :])
+        nc.sync.dma_start(q_raw[:], qT[0].rearrange("(p t) q -> p t q", t=PACK))
 
         zero = pool.tile([P, 1], F32, name="zero")
         zero_bias = pool.tile([P, 1], F32, name="zero_bias")
@@ -54,104 +52,100 @@ def tile_attend_pre_gatekey_f_topk_kernel(tc, qT, kT, gT, offs, offs2, out):
 
         gates = [pool.tile([P, N], F32, name="gates%d" % t) for t in range(PACK)]
         u_low = pool.tile([P, 2, N], F32, name="u_low")
-        u_high = {}
-        for i, j in HELD:
-            shared = pool.tile([P, 3, WIDTHS[i]], F32, name="u_shared%d" % i)
-            u_high[i] = shared[:, 1:3, :]
-            u_high[j] = shared[:, 0:2, 0 : WIDTHS[j]]
-        for j in range(PIECES):
-            if j not in u_high:
-                alone = pool.tile([P, 2, WIDTHS[j]], F32, name="u_alone%d" % j)
-                u_high[j] = alone[:]
-        u_woven = [pool.tile([P, WIDTHS[j], PACK], BF16, name="u_woven%d" % j, align_bytes=64) for j in range(PIECES)]
+        u_high = [pool.tile([P, 2, W], F32, name="u_high%d" % j) for j in range(PIECES)]
+        widths = [N, 2 * W]
+        woven = [pool.tile([P, w, PACK], BF16, name="woven%d" % g, align_bytes=64) for g, w in enumerate(widths)]
+        codes = [pool.tile([P, w], U32, name="codes%d" % g, align_bytes=64) for g, w in enumerate(widths)]
+        scales = [pool.tile([P, w], U8, name="scales%d" % g, align_bytes=64) for g, w in enumerate(widths)]
+        u_woven = [woven[0][:, j * W : (j + 1) * W, :] for j in range(3)] + [woven[1][:, 0:W, :]]
+        q_cols = [slice(3 * W, 4 * W), slice(W, 2 * W)]
 
         def gather_gates(t):
             nc.vector.tensor_copy(gates[t][:], g_pair[t // 2][:, t % 2, :].indirect(gate_list[:]))
 
         def gather_high(t, j):
-            cols = slice(STARTS[j], STARTS[j] + WIDTHS[j])
-            entries = key_list[:, STARTS[j] // 16 : (STARTS[j] + WIDTHS[j]) // 16]
+            cols = slice(j * W, (j + 1) * W)
+            entries = key_list[:, j * W // 16 : (j + 1) * W // 16]
             nc.vector.tensor_tensor(u_high[j][:, t - 2, :], k_plane[t][:].indirect(entries), gates[t][:, cols], MULT)
 
         gather_gates(0)
         gather_gates(1)
         nc.vector.tensor_tensor(u_low[:, 0, :], k_plane[0][:].indirect(key_list[:]), gates[0][:], MULT)
 
-        q_woven = pool.tile([P, NQ, PACK], BF16, name="q_woven", align_bytes=64)
-        q_codes = pool.tile([P, NQ], U32, name="q_codes", align_bytes=64)
-        q_scales = pool.tile([P, NQ], U8, name="q_scales", align_bytes=64)
-        nc.scalar.copy(q_woven[:], q_raw[:].rearrange("p t q -> p q t"))
 
         gather_gates(2)
         gather_gates(3)
-        nc.vector.quantize_mx(
-            out=q_codes[:].bitcast(FP8X4), scales=q_scales[:], in_=q_woven[:].rearrange("p q t -> p (q t)")
-        )
         nc.vector.tensor_tensor(u_low[:, 1, :], k_plane[1][:].indirect(key_list[:]), gates[1][:], MULT)
         for j in range(PIECES):
-            cols = slice(STARTS[j], STARTS[j] + WIDTHS[j])
+            cols = slice(j * W, (j + 1) * W)
             nc.scalar.copy(u_woven[j][:, :, 0:2], u_low[:, :, cols].rearrange("p t c -> p c t"))
 
         for j in range(PIECES):
             gather_high(2, j)
 
-        u_codes = [pool.tile([P, WIDTHS[j]], U32, name="u_codes%d" % j, align_bytes=64) for j in range(PIECES)]
-        u_scales = [pool.tile([P, WIDTHS[j]], U8, name="u_scales%d" % j, align_bytes=64) for j in range(PIECES)]
-        scores = [psum.tile([P, QB, WIDTHS[j]], F32, name="scores%d" % j) for j in range(PIECES)]
-        capped = [pool.tile([P, QB, WIDTHS[j]], F32, name="capped%d" % j) for j in range(PIECES)]
-        result = [pool.tile([P, QB, WIDTHS[j]], F32, name="result%d" % j) for j in range(PIECES)]
-        out_rows = out[0].rearrange("(b p) n -> p b n", p=P)
+        scores = [psum.tile([P, 2 * W], F32, name="scores%d" % j) for j in range(4)]
+        capped = [pool.tile([P, 2 * W], F32, name="capped%d" % j) for j in range(4)]
+        result = [pool.tile([P, 2 * W], F32, name="result%d" % j) for j in range(4)]
 
         def weave(j, copy):
-            copy(u_woven[j][:, :, 2:4], u_high[j].rearrange("p t c -> p c t"))
+            copy(u_woven[j][:, :, 2:4], u_high[j][:].rearrange("p t c -> p c t"))
+
+        def weave_q(b, copy):
+            copy(woven[b][:, q_cols[b], :], q_raw[:, :, b * P : (b + 1) * P].rearrange("p t q -> p q t"))
+
+        def quantise(g):
+            nc.vector.quantize_mx(
+                out=codes[g][:].bitcast(FP8X4), scales=scales[g][:], in_=woven[g][:].rearrange("p c t -> p (c t)")
+            )
+
+        def product(dst, b, g, cols):
+            nc.tensor.matmul_mx(
+                out=dst,
+                lhsT=codes[b][:, q_cols[b]].bitcast(FP8X4),
+                lhsT_scale=scales[b][:, q_cols[b]],
+                rhs=codes[g][:, cols].bitcast(FP8X4),
+                rhs_scale=scales[g][:, cols],
+                start=True,
+                stop=True,
+            )
 
         def multiply(j):
-            nc.vector.quantize_mx(
-                out=u_codes[j][:].bitcast(FP8X4),
-                scales=u_scales[j][:],
-                in_=u_woven[j][:].rearrange("p c t -> p (c t)"),
-            )
-            for b in range(QB):
-                rows = slice(b * P, (b + 1) * P)
-                nc.tensor.matmul_mx(
-                    out=scores[j][:, b, :],
-                    lhsT=q_codes[:, rows].bitcast(FP8X4),
-                    lhsT_scale=q_scales[:, rows],
-                    rhs=u_codes[j][:].bitcast(FP8X4),
-                    rhs_scale=u_scales[j][:],
-                    start=True,
-                    stop=True,
-                )
+            b, half = divmod(j, 2)
+            if half == 0:
+                product(scores[j][:], b, 0, slice(0, 2 * W))
+            else:
+                product(scores[j][:, 0:W], b, 0, slice(2 * W, 3 * W))
+                product(scores[j][:, W : 2 * W], b, 1, slice(0, W))
 
         def cap(j):
             nc.scalar.activation(capped[j][:], scores[j][:], TANH, bias=zero_bias[:], scale=1.0 / CAP)
 
         def store(j):
+            b, half = divmod(j, 2)
             nc.vector.tensor_scalar_mul(result[j][:], capped[j][:], CAP)
-            nc.sync.dma_start(out_rows[:, :, STARTS[j] : STARTS[j] + WIDTHS[j]], result[j][:])
+            nc.sync.dma_start(out[0, b * P : (b + 1) * P, half * 2 * W : (half + 1) * 2 * W], result[j][:])
 
         gather_high(3, 0)
         weave(0, nc.scalar.copy)
         gather_high(3, 1)
         weave(1, nc.scalar.copy)
         gather_high(3, 2)
-        weave(2, nc.scalar.copy)
-        multiply(0)
         gather_high(3, 3)
-        weave(3, nc.scalar.copy)
+        weave_q(0, nc.scalar.copy)
+        weave_q(1, nc.scalar.copy)
+        weave(2, nc.vector.tensor_copy)
+        weave(3, nc.vector.tensor_copy)
+        quantise(0)
+        quantise(1)
+        multiply(0)
         multiply(1)
-        gather_high(3, 4)
-        weave(4, nc.vector.tensor_copy)
         multiply(2)
         multiply(3)
-        multiply(4)
         cap(0)
         cap(1)
         cap(2)
         cap(3)
-        cap(4)
         store(0)
         store(1)
         store(2)
         store(3)
-        store(4)

@@ -83,15 +83,19 @@ def tile_attend_pre_gatekey_f_topk_kernel(tc, qT, kT, gT, offs, offs2, out):
         for j in range(PIECES):
             gather_high(2, j)
 
-        scores = [psum.tile([P, 2 * W], F32, name="scores%d" % j) for j in range(4)]
-        capped = [pool.tile([P, 2 * W], F32, name="capped%d" % j) for j in range(4)]
-        result = [pool.tile([P, 2 * W], F32, name="result%d" % j) for j in range(4)]
+        units = [(0, 0, 128), (0, 128, 384), (1, 0, 256), (1, 256, 512), (0, 384, 512)]
+        scores = [psum.tile([P, c1 - c0], F32, name="scores%d" % j) for j, (b, c0, c1) in enumerate(units)]
+        capped = [pool.tile([P, c1 - c0], F32, name="capped%d" % j) for j, (b, c0, c1) in enumerate(units)]
+        result = [pool.tile([P, c1 - c0], F32, name="result%d" % j) for j, (b, c0, c1) in enumerate(units)]
 
         def weave(j, copy):
             copy(u_woven[j][:, :, 2:4], u_high[j][:].rearrange("p t c -> p c t"))
 
         def weave_q(b, copy):
-            copy(woven[b][:, q_cols[b], :], q_raw[:, :, b * P : (b + 1) * P].rearrange("p t q -> p q t"))
+            copy(
+                woven[b][:, q_cols[b], :].rearrange("p (c i) t -> p c t i", i=4),
+                q_raw[:, :, b * P : (b + 1) * P].rearrange("p t (c i) -> p c t i", i=4),
+            )
 
         def quantise(g):
             nc.vector.quantize_mx(
@@ -110,20 +114,20 @@ def tile_attend_pre_gatekey_f_topk_kernel(tc, qT, kT, gT, offs, offs2, out):
             )
 
         def multiply(j):
-            b, half = divmod(j, 2)
-            if half == 0:
-                product(scores[j][:], b, 0, slice(0, 2 * W))
-            else:
-                product(scores[j][:, 0:W], b, 0, slice(2 * W, 3 * W))
-                product(scores[j][:, W : 2 * W], b, 1, slice(0, W))
+            b, c0, c1 = units[j]
+            cut = 3 * W
+            if c0 < cut:
+                product(scores[j][:, 0 : min(c1, cut) - c0], b, 0, slice(c0, min(c1, cut)))
+            if c1 > cut:
+                product(scores[j][:, cut - c0 : c1 - c0], b, 1, slice(0, W))
 
         def cap(j):
             nc.scalar.activation(capped[j][:], scores[j][:], TANH, bias=zero_bias[:], scale=1.0 / CAP)
 
         def store(j):
-            b, half = divmod(j, 2)
+            b, c0, c1 = units[j]
             nc.vector.tensor_scalar_mul(result[j][:], capped[j][:], CAP)
-            nc.sync.dma_start(out[0, b * P : (b + 1) * P, half * 2 * W : (half + 1) * 2 * W], result[j][:])
+            nc.sync.dma_start(out[0, b * P : (b + 1) * P, c0:c1], result[j][:])
 
         gather_high(3, 0)
         weave(0, nc.scalar.copy)
@@ -141,11 +145,14 @@ def tile_attend_pre_gatekey_f_topk_kernel(tc, qT, kT, gT, offs, offs2, out):
         multiply(1)
         multiply(2)
         multiply(3)
+        multiply(4)
         cap(0)
         cap(1)
         cap(2)
         cap(3)
+        cap(4)
         store(0)
         store(1)
         store(2)
         store(3)
+        store(4)

from contextlib import ExitStack

import concourse.mybir as mybir

D, T, G, N, NQ = 512, 2048, 1024, 512, 256
FLOPS = 2 * D * N * NQ

F32 = mybir.dt.float32
BF16 = mybir.dt.bfloat16
U32 = mybir.dt.uint32
U16 = mybir.dt.uint16
U8 = mybir.dt.uint8
FP8X4 = mybir.dt.float8_e4m3fn_x4
MULT = mybir.AluOpType.mult
TANH = mybir.ActivationFunctionType.Tanh

P = 128
PACK = 4
CAP = 15.0
PIECES = 4
W = N // PIECES
QB = NQ // P


def tile_attend_pre_gatekey_f_topk_kernel(tc, qT, kT, gT, offs, offs2, out):
    nc = tc.nc
    with ExitStack() as ctx:
        pool = ctx.enter_context(tc.tile_pool(name="pool", bufs=1))
        psum = ctx.enter_context(tc.psum_pool(name="psum", bufs=1))

        key_list = pool.tile([P, N // 16], U16, name="key_list")
        gate_list = pool.tile([P, N // 16], U16, name="gate_list")
        k_rows = kT.rearrange("(p t) n -> p t n", t=PACK)
        g_rows = gT.rearrange("(p t) n -> p t n", t=PACK)
        k_plane = [pool.tile([P, T], F32, name="k_plane%d" % t) for t in range(PACK)]
        g_pair = [pool.tile([P, 2, G], F32, name="g_pair%d" % h) for h in range(2)]
        q_raw = pool.tile([P, PACK, NQ], F32, name="q_raw")

        nc.sync.dma_start(g_pair[0][:], g_rows[:, 0:2, :])
        nc.sync.dma_start(gate_list[:], offs2)
        nc.sync.dma_start(key_list[:], offs)
        nc.sync.dma_start(k_plane[0][:], k_rows[:, 0, :])
        nc.sync.dma_start(g_pair[1][:], g_rows[:, 2:4, :])
        for t in range(1, PACK):
            nc.sync.dma_start(k_plane[t][:], k_rows[:, t, :])
        nc.sync.dma_start(q_raw[:], qT[0].rearrange("(p t) q -> p t q", t=PACK))

        zero = pool.tile([P, 1], F32, name="zero")
        zero_bias = pool.tile([P, 1], F32, name="zero_bias")
        nc.vector.memset(zero[:], 0.0)
        nc.scalar.activation(zero_bias[:], zero[:], TANH)

        gates = [pool.tile([P, N], F32, name="gates%d" % t) for t in range(PACK)]
        u_low = pool.tile([P, 2, N], F32, name="u_low")
        u_high = [pool.tile([P, 2, W], F32, name="u_high%d" % j) for j in range(PIECES)]
        widths = [N, 2 * W]
        woven = [pool.tile([P, w, PACK], BF16, name="woven%d" % g, align_bytes=64) for g, w in enumerate(widths)]
        codes = [pool.tile([P, w], U32, name="codes%d" % g, align_bytes=64) for g, w in enumerate(widths)]
        scales = [pool.tile([P, w], U8, name="scales%d" % g, align_bytes=64) for g, w in enumerate(widths)]
        u_woven = [woven[0][:, j * W : (j + 1) * W, :] for j in range(3)] + [woven[1][:, 0:W, :]]
        q_cols = [slice(3 * W, 4 * W), slice(W, 2 * W)]

        def gather_gates(t):
            nc.vector.tensor_copy(gates[t][:], g_pair[t // 2][:, t % 2, :].indirect(gate_list[:]))

        def gather_high(t, j):
            cols = slice(j * W, (j + 1) * W)
            entries = key_list[:, j * W // 16 : (j + 1) * W // 16]
            nc.vector.tensor_tensor(u_high[j][:, t - 2, :], k_plane[t][:].indirect(entries), gates[t][:, cols], MULT)

        gather_gates(0)
        gather_gates(1)
        nc.vector.tensor_tensor(u_low[:, 0, :], k_plane[0][:].indirect(key_list[:]), gates[0][:], MULT)


        gather_gates(2)
        gather_gates(3)
        nc.vector.tensor_tensor(u_low[:, 1, :], k_plane[1][:].indirect(key_list[:]), gates[1][:], MULT)
        for j in range(PIECES):
            cols = slice(j * W, (j + 1) * W)
            nc.scalar.copy(u_woven[j][:, :, 0:2], u_low[:, :, cols].rearrange("p t c -> p c t"))

        for j in range(PIECES):
            gather_high(2, j)

        units = [(0, 0, 128), (0, 128, 384), (1, 0, 256), (1, 256, 512), (0, 384, 512)]
        scores = [psum.tile([P, c1 - c0], F32, name="scores%d" % j) for j, (b, c0, c1) in enumerate(units)]
        capped = [pool.tile([P, c1 - c0], F32, name="capped%d" % j) for j, (b, c0, c1) in enumerate(units)]
        result = [pool.tile([P, c1 - c0], F32, name="result%d" % j) for j, (b, c0, c1) in enumerate(units)]

        def weave(j, copy):
            copy(u_woven[j][:, :, 2:4], u_high[j][:].rearrange("p t c -> p c t"))

        def weave_q(b, copy):
            copy(
                woven[b][:, q_cols[b], :].rearrange("p (c i) t -> p c t i", i=4),
                q_raw[:, :, b * P : (b + 1) * P].rearrange("p t (c i) -> p c t i", i=4),
            )

        def quantise(g):
            nc.vector.quantize_mx(
                out=codes[g][:].bitcast(FP8X4), scales=scales[g][:], in_=woven[g][:].rearrange("p c t -> p (c t)")
            )

        def product(dst, b, g, cols):
            nc.tensor.matmul_mx(
                out=dst,
                lhsT=codes[b][:, q_cols[b]].bitcast(FP8X4),
                lhsT_scale=scales[b][:, q_cols[b]],
                rhs=codes[g][:, cols].bitcast(FP8X4),
                rhs_scale=scales[g][:, cols],
                start=True,
                stop=True,
            )

        def multiply(j):
            b, c0, c1 = units[j]
            cut = 3 * W
            if c0 < cut:
                product(scores[j][:, 0 : min(c1, cut) - c0], b, 0, slice(c0, min(c1, cut)))
            if c1 > cut:
                product(scores[j][:, cut - c0 : c1 - c0], b, 1, slice(0, W))

        def cap(j):
            nc.scalar.activation(capped[j][:], scores[j][:], TANH, bias=zero_bias[:], scale=1.0 / CAP)

        def store(j):
            b, c0, c1 = units[j]
            nc.vector.tensor_scalar_mul(result[j][:], capped[j][:], CAP)
            nc.sync.dma_start(out[0, b * P : (b + 1) * P, c0:c1], result[j][:])

        gather_high(3, 0)
        weave(0, nc.scalar.copy)
        gather_high(3, 1)
        weave(1, nc.scalar.copy)
        gather_high(3, 2)
        gather_high(3, 3)
        weave_q(0, nc.scalar.copy)
        weave_q(1, nc.scalar.copy)
        weave(2, nc.vector.tensor_copy)
        weave(3, nc.vector.tensor_copy)
        quantise(0)
        quantise(1)
        multiply(0)
        multiply(1)
        multiply(2)
        multiply(3)
        multiply(4)
        cap(0)
        cap(1)
        cap(2)
        cap(3)
        cap(4)
        store(0)
        store(1)
        store(2)
        store(3)
        store(4)
